import numpy as np
import ml_dtypes


def mxq(x, axis, fmt="e4m3"):
    dtype, down = {"e4m3": (ml_dtypes.float8_e4m3fn, 7), "e5m2": (ml_dtypes.float8_e5m2, 14)}[fmt]
    v = np.moveaxis(np.asarray(x, np.float32).astype(ml_dtypes.bfloat16).astype(np.float64), axis, -1)
    blocks = v.reshape(v.shape[:-1] + (-1, 32))
    amax = np.abs(blocks).max(-1, keepdims=True)
    byte = np.maximum(np.where(amax > 0, np.frexp(amax)[1] - 1 + 127, 0) - down, 1)
    scale = np.exp2(byte - 127.0)
    codes = (blocks / scale).astype(np.float32).astype(dtype).astype(np.float64)
    return np.moveaxis((codes * scale).reshape(v.shape), -1, axis)


WIDE = False


def mx_kscale(k):
    if not WIDE:
        return np.ones(k)
    levels = np.array([10, -10, 5, -5, 0])
    if k % 512:
        return np.exp2(np.random.permutation(np.resize(levels, k // 32))).repeat(32)
    a = np.empty((k // 512, 16))
    for p in range(k // 512):
        a[p, :8] = np.random.permutation(np.resize(levels, 8))
        for g in range(8):
            far = levels[np.abs(levels - a[p, g]) >= 10]
            a[p, g + 8] = far[np.random.randint(len(far))]
    return np.exp2(a.ravel()).repeat(32)


def f64(x):
    return np.asarray(x).astype(np.float64)


def striped(idx):
    return np.tile(idx.reshape(-1, 16).T, (8, 1)).astype(np.uint16)


def unstriped(offs):
    return offs[:16].T.reshape(-1).astype(np.int64)


E2M1 = np.array([0.0, 0.5, 1.0, 1.5, 2.0, 3.0, 4.0, 6.0, -0.0, -0.5, -1.0, -1.5, -2.0, -3.0, -4.0, -6.0])


def pack_weight(w, fmt):
    k, n = w.shape
    w = f64(np.asarray(w, np.float32).astype(ml_dtypes.bfloat16)).reshape(k // 32, 32, n)
    amax = np.abs(w).max(1)
    if fmt == "e4m3":
        byte = np.frexp(amax)[1] - 1 + 127 - 7
    else:
        mant, ex = np.frexp(amax / 6.0)
        byte = np.where(mant > 0.5, ex, ex - 1) + 127
    byte = np.clip(np.where(amax > 0, byte, 1), 1, 254)
    scaled = (w * np.exp2(127.0 - byte)[:, None, :]).reshape(k, n).astype(np.float32)
    by_word = np.ascontiguousarray(scaled.reshape(k // 512, 128, 4, n).transpose(0, 1, 3, 2))
    if fmt == "e4m3":
        words = by_word.astype(ml_dtypes.float8_e4m3fn).view(np.uint8)
    else:
        c = by_word.astype(ml_dtypes.float4_e2m1fn).view(np.uint8) & 0xF
        words = (c[..., 0::2] | (c[..., 1::2] << 4)).reshape(k // 512, 128, 2 * n)
    return np.ascontiguousarray(words), np.ascontiguousarray(byte.astype(np.uint8).reshape(k // 512, 16, n))


def unpack_weight(words, scales, fmt):
    g, _, n = scales.shape
    words = np.ascontiguousarray(words).reshape(g, 128, n, -1)
    if fmt == "e4m3":
        vals = words.view(ml_dtypes.float8_e4m3fn).astype(np.float64)
    else:
        nib = np.empty((g, 128, n, 4), np.uint8)
        nib[..., 0::2] = words & 0xF
        nib[..., 1::2] = words >> 4
        vals = E2M1[nib]
    vals = vals * np.repeat(np.exp2(scales.astype(np.float64) - 127.0), 8, axis=1)[..., None]
    return vals.transpose(0, 1, 3, 2).reshape(g * 512, n)


def gelu(v):
    return 0.5 * v * (1.0 + np.tanh(np.sqrt(2.0 / np.pi) * (v + 0.044715 * v**3)))


K, H, N, T, S, P, P2 = 1536, 1024, 768, 4096, 1024, 512, 256

def setup_inputs():
    n = np.random.standard_normal
    s = mx_kscale(K)[:, None]
    u = mx_kscale(H)[:, None]
    tab_words, tab_scales = pack_weight(n((K, T)) * s, "e4m3")
    w2_words, w2_scales = pack_weight(n((H, N)) / np.sqrt(H) / u, "e2m1")
    return {
        "tab_words": tab_words, "tab_scales": tab_scales,
        "offs": striped(np.random.permutation(T)[:S]),
        "pos1": striped(np.random.permutation(S)[:P]),
        "pos2": striped(np.random.permutation(S)[:P]),
        "pos3": striped(np.random.permutation(P)[:P2]),
        "pos4": striped(np.random.permutation(P)[:P2]),
        "w1": (1.5 * n((K, H)) / np.sqrt(K) / s).astype(np.float32),
        "gain": ((1.0 + 0.7 * n(H)) * u[:, 0]).astype(np.float32),
        "w2_words": w2_words, "w2_scales": w2_scales,
    }

def reference(tab_words, tab_scales, offs, pos1, pos2, pos3, pos4, w1, gain, w2_words, w2_scales):
    v = unpack_weight(tab_words, tab_scales, "e4m3")[:, unstriped(offs)]
    lin = mxq(f64(w1), 0, "e4m3").T @ v
    act = 0.5 * lin * (1.0 + np.tanh(np.sqrt(2.0 / np.pi) * (lin + 0.044715 * lin ** 3)))
    h = act * f64(gain)[:, None]
    top, bottom = unstriped(pos1), unstriped(pos2)
    both = np.tanh(act[:, top] + act[:, bottom])
    larger = np.maximum(h[:, top], h[:, bottom])
    z = mxq(both * larger, 0, "e4m3")
    y = unpack_weight(w2_words, w2_scales, "e2m1").T @ z
    return y[:, unstriped(pos3)] - y[:, unstriped(pos4)]

@@ -1,0 +1,323 @@
+from contextlib import ExitStack
+
+import concourse.mybir as mybir
+from concourse.masks import make_identity
+
+K, H, N, T, S, PAIRS, DIFFS = 1536, 1024, 768, 4096, 1024, 512, 256
+FLOPS = 2 * K * H * S + 2 * H * N * PAIRS
+
+F32 = mybir.dt.float32
+BF16 = mybir.dt.bfloat16
+I32 = mybir.dt.int32
+U32 = mybir.dt.uint32
+U16 = mybir.dt.uint16
+U8 = mybir.dt.uint8
+FP8X4 = mybir.dt.float8_e4m3fn_x4
+FP4X4 = mybir.dt.float4_e2m1fn_x4
+ALU = mybir.AluOpType
+ACT = mybir.ActivationFunctionType
+
+P = 128
+PACK = 4
+K_PASS = P * PACK
+K_PASSES = K // K_PASS
+R_PASSES = H // K_PASS
+TILES = H // P
+TILES_PER_PASS = K_PASS // P
+BANK = 512
+HALVES = S // BANK
+M_CHUNKS = PAIRS // P
+M_HALF = PAIRS // 2
+N_TILES = N // P
+ACT_AT = 5 * T
+W1_CHUNKS = (1, 1, 1, 1, 2, 2)
+
+
+def tile_list_cocoa_turning_features_kernel(
+    tc, tab_words, tab_scales, offs, pos1, pos2, pos3, pos4, w1, gain, w2_words, w2_scales, out
+):
+    nc = tc.nc
+    with ExitStack() as ctx:
+        held = ctx.enter_context(tc.tile_pool(name="held", bufs=1))
+        ring2 = ctx.enter_context(tc.tile_pool(name="ring2", bufs=2))
+        ring3 = ctx.enter_context(tc.tile_pool(name="ring3", bufs=3))
+        reused = ctx.enter_context(tc.tile_pool(name="reused", bufs=1))
+        psum_lin = ctx.enter_context(tc.psum_pool(name="psum_lin", bufs=5))
+        psum_one = ctx.enter_context(tc.psum_pool(name="psum_one", bufs=1))
+        psum_z = ctx.enter_context(tc.psum_pool(name="psum_z", bufs=2))
+
+        def load_list(src, name):
+            tile = held.tile(list(src.shape), U16, name=name)
+            nc.sync.dma_start(tile[:], src)
+            return tile
+
+        def load_table_words(a):
+            if a == K_PASSES - 1:
+                tile = reused.tile([P, T], I32, name=f"tab_w{a}", align_bytes=64, offset=0)
+            else:
+                tile = held.tile([P, T], I32, name=f"tab_w{a}", align_bytes=64)
+            nc.sync.dma_start(tile[:], tab_words[a].rearrange("p t i -> p (t i)").bitcast(I32))
+            return tile
+
+        tab_s = reused.tile([P, T], U8, name="tab_s", align_bytes=64, offset=4 * T)
+        nc.vector.memset(tab_s[:].bitcast(I32), 0)
+        w2_s = held.tile([P, R_PASSES, N], U8, name="w2_s", align_bytes=64)
+        nc.vector.memset(w2_s[:].rearrange("p a n -> p (a n)").bitcast(I32), 0)
+        for quad in range(4):
+            nc.gpsimd.dma_start(
+                tab_s[32 * quad : 32 * quad + 4 * K_PASSES, :].bitcast(I32),
+                tab_scales[:, 4 * quad : 4 * quad + 4, :].bitcast(I32),
+            )
+
+        tab_w = [load_table_words(0)]
+        idx = load_list(offs, "idx")
+        p1 = load_list(pos1, "p1")
+        p2 = load_list(pos2, "p2")
+        gain_rows = held.tile([TILES, P], F32, name="gain_rows")
+        nc.sync.dma_start(gain_rows[:], gain.rearrange("(c r) -> c r", r=P))
+        tab_w.append(load_table_words(1))
+
+        w1_raw = []
+        first = 0
+        for width in W1_CHUNKS:
+            parts = []
+            for a in range(K_PASSES):
+                raw = held.tile([P, PACK, width * P], F32, name=f"w1_raw{first}_{a}")
+                rows = w1[a * K_PASS : (a + 1) * K_PASS, first * P : (first + width) * P]
+                nc.sync.dma_start(raw[:], rows.rearrange("(p j) r -> p j r", j=PACK))
+                parts.append(raw)
+            for i in range(width):
+                w1_raw.append([raw[:, :, i * P : (i + 1) * P] for raw in parts])
+            if first == 0:
+                tab_w.append(load_table_words(K_PASSES - 1))
+            first = first + width
+
+        p3 = load_list(pos3, "p3")
+        p4 = load_list(pos4, "p4")
+        w2_w = held.tile([P, R_PASSES, 2 * N], U8, name="w2_w", align_bytes=64)
+        nc.sync.dma_start(w2_w[:].bitcast(I32), w2_words.rearrange("a p c -> p a c").bitcast(I32))
+        for quad in range(4):
+            nc.sync.dma_start(
+                w2_s[32 * quad : 32 * quad + 4, :, :].bitcast(I32),
+                w2_scales[:, 4 * quad : 4 * quad + 4, :].rearrange("a r c -> r a c").bitcast(I32),
+            )
+
+        ident = held.tile([P, P], F32, name="ident")
+        make_identity(nc, ident[:])
+        gain_sq = held.tile([P, P], F32, name="gain_sq")
+        nc.gpsimd.memset(gain_sq[:], 0.0)
+        nc.vector.tensor_copy(
+            gain_sq[0:TILES, :].rearrange("c (u q e) -> c u q e", u=2, e=2),
+            gain_rows[:].rearrange("c (q u e) -> c u q e", u=2, e=2),
+        )
+        gain_t = psum_one.tile([P, M_CHUNKS, P], F32, name="gain_t", tag="larger_t")
+        nc.tensor.transpose(gain_t[:, 0, :], gain_sq[:], ident[:])
+        gain_col = held.tile([P, TILES], F32, name="gain_col")
+        nc.vector.tensor_copy(gain_col[:], gain_t[:, 0, 0:TILES])
+
+        got_w = {}
+        got_s = held.tile([P, S], U8, name="got_s", align_bytes=64)
+        cols = BANK // 16
+
+        def gather_words(a):
+            for h in range(HALVES):
+                if a == K_PASSES - 1:
+                    at = 4 * T + 4 * BANK * h
+                    tile = reused.tile([P, BANK], U32, name=f"got_w{a}_{h}", align_bytes=64, offset=at)
+                else:
+                    tile = held.tile([P, BANK], U32, name=f"got_w{a}_{h}", align_bytes=64)
+                window = tab_w[a][:].bitcast(U32)
+                nc.vector.tensor_copy(tile[:], window.indirect(idx[:, h * cols : (h + 1) * cols]))
+                got_w[a, h] = tile
+
+        for a in range(K_PASSES - 1):
+            gather_words(a)
+        nc.vector.tensor_copy(got_s[:], tab_s[:].indirect(idx[:]))
+        gather_words(K_PASSES - 1)
+
+        w1_q, act, top, bottom, gained, larger_t, both_t, z_t, z_q = {}, {}, {}, {}, {}, {}, {}, {}, {}
+        sum_t, woven = {}, {}
+
+        def quantise_w1(c, pieces):
+            rounded = held.tile([P, K_PASSES, K_PASS], BF16, name="w1_bf", align_bytes=64)
+            if c == 0:
+                codes = held.tile([P, K_PASSES * P], U32, name="w1_codes_first", align_bytes=64)
+            else:
+                codes = reused.tile([P, K_PASSES * P], U32, name="w1_codes", align_bytes=64, offset=0, bufs=3)
+            scales = ring3.tile([P, K_PASSES * P], U8, name="w1_scales", align_bytes=64)
+            step = K_PASSES // pieces
+            for a in range(K_PASSES):
+                nc.scalar.copy(
+                    rounded[:, a, :].rearrange("p (u q e j) -> p u q j e", u=2, e=2, j=PACK),
+                    w1_raw[c][a].rearrange("p j (q u e) -> p u q j e", u=2, e=2),
+                )
+                if (a + 1) % step == 0:
+                    a0 = a + 1 - step
+                    nc.vector.quantize_mx(
+                        out=codes[:, a0 * P : (a + 1) * P].bitcast(FP8X4),
+                        scales=scales[:, a0 * P : (a + 1) * P],
+                        in_=rounded[:, a0 : a + 1, :].rearrange("p a x -> p (a x)"),
+                    )
+            w1_q[c] = (codes, scales)
+
+        def first_stage(c):
+            codes, scales = w1_q[c]
+            act[c] = reused.tile([P, S], F32, name="act", offset=ACT_AT, bufs=2)
+            lin = [psum_lin.tile([P, BANK], F32, name="lin", tag="acc") for h in range(HALVES)]
+            for a in range(K_PASSES):
+                for h in range(HALVES):
+                    nc.tensor.matmul_mx(
+                        out=lin[h][:],
+                        lhsT=codes[:, a * P : (a + 1) * P].bitcast(FP8X4),
+                        lhsT_scale=scales[:, a * P : (a + 1) * P],
+                        rhs=got_w[a, h][:].bitcast(FP8X4),
+                        rhs_scale=got_s[4 * a :, h * BANK : (h + 1) * BANK],
+                        start=(a == 0),
+                        stop=(a == K_PASSES - 1),
+                    )
+            for h in range(HALVES):
+                nc.scalar.activation(act[c][:, h * BANK : (h + 1) * BANK], lin[h][:], ACT.Gelu_apprx_tanh)
+
+        def gather_pairs(piece):
+            c, k0, k1 = piece
+            width = (k1 - k0) * P
+            entries = slice(k0 * P // 16, k1 * P // 16)
+            if k0 > 0:
+                bottom[piece] = held.tile([P, width], F32, name="bottom_late", tag="handed_on")
+            else:
+                bottom[piece] = ring2.tile([P, width], F32, name="bottom")
+            nc.vector.tensor_copy(bottom[piece][:], act[c][:].indirect(p2[:, entries]))
+            if k1 < M_CHUNKS:
+                gained[piece] = held.tile([P, width], F32, name="gained_early", tag="handed_on")
+            else:
+                gained[piece] = ring2.tile([P, width], F32, name="gained")
+            nc.scalar.activation(gained[piece][:], bottom[piece][:], ACT.Copy, scale=gain_col[:, c : c + 1])
+            top[piece] = ring2.tile([P, width], F32, name="top")
+            nc.vector.tensor_copy(top[piece][:], act[c][:].indirect(p1[:, entries]))
+
+        def add_turned(piece):
+            c, k0, k1 = piece
+            sum_t[piece] = psum_z.tile([P, k1 - k0, P], F32, name="sum_t")
+            steps = [(part, k) for part in (bottom[piece], top[piece]) for k in range(k1 - k0)]
+            for i, (part, k) in enumerate(steps):
+                nc.tensor.matmul(
+                    sum_t[piece][:, k, :],
+                    part[:, k * P : (k + 1) * P],
+                    ident[:],
+                    start=(i == 0),
+                    stop=(i == len(steps) - 1),
+                    is_transpose=True,
+                )
+
+        def take_larger(piece):
+            c, k0, k1 = piece
+            larger = ring2.tile([P, (k1 - k0) * P], F32, name="larger")
+            nc.vector.scalar_tensor_tensor(
+                larger[:], top[piece][:], gain_col[:, c : c + 1], gained[piece][:], ALU.mult, ALU.max
+            )
+            larger_t[piece] = psum_one.tile([P, k1 - k0, P], F32, name="larger_t", tag="larger_t")
+            for k in range(k1 - k0):
+                nc.tensor.transpose(larger_t[piece][:, k, :], larger[:, k * P : (k + 1) * P], ident[:])
+
+        def take_tanh(piece):
+            c, k0, k1 = piece
+            both_t[piece] = ring2.tile([P, k1 - k0, P], F32, name="both_t")
+            nc.scalar.activation(both_t[piece][:], sum_t[piece][:], ACT.Tanh)
+
+        def multiply(piece):
+            c, k0, k1 = piece
+            b, i = divmod(c, TILES_PER_PASS)
+            for k in range(k0, k1, 2):
+                j = k // 2
+                if i == 0:
+                    z_t[b, j] = held.tile([P, 2, 2, 2 * P], BF16, name=f"z_t{b}_{j}")
+                nc.vector.tensor_tensor(
+                    z_t[b, j][:, :, :, 64 * i : 64 * (i + 1)],
+                    larger_t[piece][:, k - k0 : k - k0 + 2, :].rearrange("p k (u x) -> p k u x", u=2),
+                    both_t[piece][:, k - k0 : k - k0 + 2, :].rearrange("p k (u x) -> p k u x", u=2),
+                    ALU.mult,
+                )
+
+        def weave_z(b, j):
+            words = z_t[b, j][:].rearrange("p k u x -> p (k u x)").bitcast(F32)
+            turned = psum_lin.tile([P, 2, 2, P], F32, name="turned", tag="acc")
+            for k in range(2):
+                for u in range(2):
+                    at = (2 * k + u) * P
+                    nc.tensor.transpose(turned[:, k, u, :], words[:, at : at + P], ident[:])
+            woven[b, j] = held.tile([P, M_HALF * PACK], BF16, name=f"woven{b}_{j}", align_bytes=64)
+            nc.scalar.copy(
+                woven[b, j][:].bitcast(F32).rearrange("p (k m u) -> p k m u", k=2, u=2),
+                turned[:].rearrange("p k u m -> p k m u"),
+            )
+
+        def quantise_z(b, j):
+            at = ACT_AT + 4 * S + 4 * M_HALF * (2 * b + j)
+            codes = reused.tile([P, M_HALF], U32, name=f"z_codes{b}_{j}", align_bytes=64, offset=at)
+            scales = held.tile([P, M_HALF], U8, name=f"z_scales{b}_{j}", align_bytes=64)
+            nc.vector.quantize_mx(out=codes[:].bitcast(FP8X4), scales=scales[:], in_=woven[b, j][:])
+            z_q[b, j] = (codes, scales)
+
+        last = TILES - 1
+        pieces = [(c, 0, M_CHUNKS) for c in range(last)] + [(last, 0, 2), (last, 2, M_CHUNKS)]
+        quantise_w1(0, 1)
+        first_stage(0)
+        quantise_w1(1, K_PASSES)
+        quantise_w1(2, 1)
+        for i, piece in enumerate(pieces):
+            c = piece[0]
+            gather_pairs(piece)
+            add_turned(piece)
+            if i > 0:
+                multiply(pieces[i - 1])
+            take_larger(piece)
+            if c + 1 < TILES:
+                first_stage(c + 1)
+            if c + 3 < TILES:
+                quantise_w1(c + 3, 1)
+            take_tanh(piece)
+            if c == TILES_PER_PASS + 1:
+                weave_z(0, 0)
+                weave_z(0, 1)
+        weave_z(1, 0)
+        multiply(pieces[-1])
+        weave_z(1, 1)
+        quantise_z(1, 0)
+        quantise_z(1, 1)
+        quantise_z(0, 0)
+        quantise_z(0, 1)
+
+        y = {}
+
+        def second_stage(n):
+            y[n] = held.tile([P, PAIRS], F32, name=f"y{n}")
+            for j in range(2):
+                acc = psum_lin.tile([P, M_HALF], F32, name="y_acc", tag="acc")
+                for b in range(R_PASSES):
+                    codes, scales = z_q[b, j]
+                    nc.tensor.matmul_mx(
+                        out=acc[:],
+                        lhsT=w2_w[:, b, 2 * n * P : 2 * (n + 1) * P].bitcast(FP4X4),
+                        lhsT_scale=w2_s[:, b, n * P : (n + 1) * P],
+                        rhs=codes[:].bitcast(FP8X4),
+                        rhs_scale=scales[:],
+                        start=(b == 0),
+                        stop=(b == R_PASSES - 1),
+                    )
+                nc.scalar.copy(y[n][:, j * M_HALF : (j + 1) * M_HALF], acc[:])
+
+        def gather_later(n):
+            later = ring3.tile([P, DIFFS], F32, name="later")
+            nc.vector.tensor_copy(later[:], y[n][:].indirect(p4[:]))
+            return later
+
+        second_stage(0)
+        later = gather_later(0)
+        for n in range(N_TILES):
+            if n + 1 < N_TILES:
+                second_stage(n + 1)
+                upcoming = gather_later(n + 1)
+            diff = ring3.tile([P, DIFFS], F32, name="diff")
+            nc.vector.tensor_tensor(diff[:], y[n][:].indirect(p3[:]), later[:], ALU.subtract)
+            nc.sync.dma_start(out[n * P : (n + 1) * P, :], diff[:])
+            later = upcoming

@@ -29,6 +29,7 @@ HALVES = S // BANK
 M_CHUNKS = PAIRS // P
 M_HALF = PAIRS // 2
 N_TILES = N // P
+LAST_CUTS = ((0, 2), (2, 3), (3, 4))
 ACT_AT = 5 * T
 W1_CHUNKS = (1, 1, 1, 1, 2, 2)
 
@@ -42,9 +43,7 @@ def tile_list_cocoa_turning_features_kernel(
         ring2 = ctx.enter_context(tc.tile_pool(name="ring2", bufs=2))
         ring3 = ctx.enter_context(tc.tile_pool(name="ring3", bufs=3))
         reused = ctx.enter_context(tc.tile_pool(name="reused", bufs=1))
-        psum_lin = ctx.enter_context(tc.psum_pool(name="psum_lin", bufs=5))
-        psum_one = ctx.enter_context(tc.psum_pool(name="psum_one", bufs=1))
-        psum_z = ctx.enter_context(tc.psum_pool(name="psum_z", bufs=2))
+        psum = ctx.enter_context(tc.psum_pool(name="psum", bufs=4))
 
         def load_list(src, name):
             tile = held.tile(list(src.shape), U16, name=name)
@@ -59,40 +58,37 @@ def tile_list_cocoa_turning_features_kernel(
             nc.sync.dma_start(tile[:], tab_words[a].rearrange("p t i -> p (t i)").bitcast(I32))
             return tile
 
-        tab_s = reused.tile([P, T], U8, name="tab_s", align_bytes=64, offset=4 * T)
-        nc.vector.memset(tab_s[:].bitcast(I32), 0)
+        tab_s = reused.tile([P, T // 4], I32, name="tab_s", align_bytes=64, offset=4 * T)
+        nc.vector.memset(tab_s[:], 0)
         w2_s = held.tile([P, R_PASSES, N], U8, name="w2_s", align_bytes=64)
         nc.vector.memset(w2_s[:].rearrange("p a n -> p (a n)").bitcast(I32), 0)
         for quad in range(4):
             nc.gpsimd.dma_start(
-                tab_s[32 * quad : 32 * quad + 4 * K_PASSES, :].bitcast(I32),
+                tab_s[32 * quad : 32 * quad + 4 * K_PASSES, :],
                 tab_scales[:, 4 * quad : 4 * quad + 4, :].bitcast(I32),
             )
 
         tab_w = [load_table_words(0)]
         idx = load_list(offs, "idx")
+        tab_w.append(load_table_words(1))
         p1 = load_list(pos1, "p1")
         p2 = load_list(pos2, "p2")
         gain_rows = held.tile([TILES, P], F32, name="gain_rows")
         nc.sync.dma_start(gain_rows[:], gain.rearrange("(c r) -> c r", r=P))
-        tab_w.append(load_table_words(1))
 
         w1_raw = []
         first = 0
         for width in W1_CHUNKS:
-            parts = []
+            raw = held.tile([P, K_PASSES, PACK, width * P], F32, name=f"w1_raw{first}")
             for a in range(K_PASSES):
-                raw = held.tile([P, PACK, width * P], F32, name=f"w1_raw{first}_{a}")
                 rows = w1[a * K_PASS : (a + 1) * K_PASS, first * P : (first + width) * P]
-                nc.sync.dma_start(raw[:], rows.rearrange("(p j) r -> p j r", j=PACK))
-                parts.append(raw)
-            for i in range(width):
-                w1_raw.append([raw[:, :, i * P : (i + 1) * P] for raw in parts])
+                nc.sync.dma_start(raw[:, a], rows.rearrange("(p j) r -> p j r", j=PACK))
+            w1_raw.extend(raw[:, :, :, i * P : (i + 1) * P] for i in range(width))
             if first == 0:
+                p3 = load_list(pos3, "p3")
                 tab_w.append(load_table_words(K_PASSES - 1))
             first = first + width
 
-        p3 = load_list(pos3, "p3")
         p4 = load_list(pos4, "p4")
         w2_w = held.tile([P, R_PASSES, 2 * N], U8, name="w2_w", align_bytes=64)
         nc.sync.dma_start(w2_w[:].bitcast(I32), w2_words.rearrange("a p c -> p a c").bitcast(I32))
@@ -106,11 +102,8 @@ def tile_list_cocoa_turning_features_kernel(
         make_identity(nc, ident[:])
         gain_sq = held.tile([P, P], F32, name="gain_sq")
         nc.gpsimd.memset(gain_sq[:], 0.0)
-        nc.vector.tensor_copy(
-            gain_sq[0:TILES, :].rearrange("c (u q e) -> c u q e", u=2, e=2),
-            gain_rows[:].rearrange("c (q u e) -> c u q e", u=2, e=2),
-        )
-        gain_t = psum_one.tile([P, M_CHUNKS, P], F32, name="gain_t", tag="larger_t")
+        nc.vector.tensor_copy(gain_sq[0:TILES, :], gain_rows[:])
+        gain_t = psum.tile([P, M_CHUNKS, P], F32, name="gain_t", tag="bank")
         nc.tensor.transpose(gain_t[:, 0, :], gain_sq[:], ident[:])
         gain_col = held.tile([P, TILES], F32, name="gain_col")
         nc.vector.tensor_copy(gain_col[:], gain_t[:, 0, 0:TILES])
@@ -132,42 +125,42 @@ def tile_list_cocoa_turning_features_kernel(
 
         for a in range(K_PASSES - 1):
             gather_words(a)
-        nc.vector.tensor_copy(got_s[:], tab_s[:].indirect(idx[:]))
+        nc.vector.tensor_copy(got_s[:], tab_s[:].bitcast(U8).indirect(idx[:]))
         gather_words(K_PASSES - 1)
 
         w1_q, act, top, bottom, gained, larger_t, both_t, z_t, z_q = {}, {}, {}, {}, {}, {}, {}, {}, {}
-        sum_t, woven = {}, {}
+        sum_t, woven, rounded, lin = {}, {}, {}, {}
 
-        def quantise_w1(c, pieces):
-            rounded = held.tile([P, K_PASSES, K_PASS], BF16, name="w1_bf", align_bytes=64)
-            if c == 0:
-                codes = held.tile([P, K_PASSES * P], U32, name="w1_codes_first", align_bytes=64)
+        def round_w1(c, step=K_PASSES):
+            if c == 1:
+                rounded = held.tile([P, K_PASSES, K_PASS], BF16, name="w1_bf_second", tag="handed_on0", align_bytes=64)
             else:
-                codes = reused.tile([P, K_PASSES * P], U32, name="w1_codes", align_bytes=64, offset=0, bufs=3)
-            scales = ring3.tile([P, K_PASSES * P], U8, name="w1_scales", align_bytes=64)
-            step = K_PASSES // pieces
-            for a in range(K_PASSES):
+                rounded = ring2.tile([P, K_PASSES, K_PASS], BF16, name="w1_bf", align_bytes=64)
+            if c < W1_CHUNKS[0]:
+                codes = held.tile([P, K_PASSES * P], U32, name=f"w1_codes_first{c}", align_bytes=64)
+            else:
+                codes = reused.tile([P, K_PASSES * P], U32, name="w1_codes", align_bytes=64, offset=0, bufs=2)
+            scales = ring2.tile([P, K_PASSES * P], U8, name="w1_scales", align_bytes=64)
+            for a0 in range(0, K_PASSES, step):
+                a1 = a0 + step
                 nc.scalar.copy(
-                    rounded[:, a, :].rearrange("p (u q e j) -> p u q j e", u=2, e=2, j=PACK),
-                    w1_raw[c][a].rearrange("p j (q u e) -> p u q j e", u=2, e=2),
+                    rounded[:, a0:a1, :].rearrange("p a (g i j) -> p a g j i", i=4, j=PACK),
+                    w1_raw[c][:, a0:a1].rearrange("p a j (g i) -> p a g j i", i=4),
                 )
-                if (a + 1) % step == 0:
-                    a0 = a + 1 - step
-                    nc.vector.quantize_mx(
-                        out=codes[:, a0 * P : (a + 1) * P].bitcast(FP8X4),
-                        scales=scales[:, a0 * P : (a + 1) * P],
-                        in_=rounded[:, a0 : a + 1, :].rearrange("p a x -> p (a x)"),
-                    )
+                nc.vector.quantize_mx(
+                    out=codes[:, a0 * P : a1 * P].bitcast(FP8X4),
+                    scales=scales[:, a0 * P : a1 * P],
+                    in_=rounded[:, a0:a1, :].rearrange("p a x -> p (a x)"),
+                )
             w1_q[c] = (codes, scales)
 
-        def first_stage(c):
+        def first_product(c):
             codes, scales = w1_q[c]
-            act[c] = reused.tile([P, S], F32, name="act", offset=ACT_AT, bufs=2)
-            lin = [psum_lin.tile([P, BANK], F32, name="lin", tag="acc") for h in range(HALVES)]
+            lin[c] = [psum.tile([P, BANK], F32, name="lin", tag="sums") for h in range(HALVES)]
             for a in range(K_PASSES):
                 for h in range(HALVES):
                     nc.tensor.matmul_mx(
-                        out=lin[h][:],
+                        out=lin[c][h][:],
                         lhsT=codes[:, a * P : (a + 1) * P].bitcast(FP8X4),
                         lhsT_scale=scales[:, a * P : (a + 1) * P],
                         rhs=got_w[a, h][:].bitcast(FP8X4),
@@ -175,29 +168,32 @@ def tile_list_cocoa_turning_features_kernel(
                         start=(a == 0),
                         stop=(a == K_PASSES - 1),
                     )
+
+        def take_gelu(c):
+            act[c] = reused.tile([P, S], F32, name="act", offset=ACT_AT, bufs=2)
             for h in range(HALVES):
-                nc.scalar.activation(act[c][:, h * BANK : (h + 1) * BANK], lin[h][:], ACT.Gelu_apprx_tanh)
+                nc.scalar.activation(act[c][:, h * BANK : (h + 1) * BANK], lin[c][h][:], ACT.Gelu_apprx_tanh)
 
         def gather_pairs(piece):
             c, k0, k1 = piece
             width = (k1 - k0) * P
             entries = slice(k0 * P // 16, k1 * P // 16)
-            if k0 > 0:
-                bottom[piece] = held.tile([P, width], F32, name="bottom_late", tag="handed_on")
-            else:
-                bottom[piece] = ring2.tile([P, width], F32, name="bottom")
+            bottom[piece] = ring3.tile([P, width], F32, name="bottom")
             nc.vector.tensor_copy(bottom[piece][:], act[c][:].indirect(p2[:, entries]))
             if k1 < M_CHUNKS:
-                gained[piece] = held.tile([P, width], F32, name="gained_early", tag="handed_on")
+                gained[piece] = held.tile([P, width], F32, name="gained_early", tag=f"handed_on{k1}", align_bytes=64)
             else:
                 gained[piece] = ring2.tile([P, width], F32, name="gained")
             nc.scalar.activation(gained[piece][:], bottom[piece][:], ACT.Copy, scale=gain_col[:, c : c + 1])
-            top[piece] = ring2.tile([P, width], F32, name="top")
+            if k0 > 0 or c == 0:
+                top[piece] = held.tile([P, width], F32, name="top_late", tag=f"handed_on{k0}", align_bytes=64)
+            else:
+                top[piece] = ring2.tile([P, width], F32, name="top")
             nc.vector.tensor_copy(top[piece][:], act[c][:].indirect(p1[:, entries]))
 
         def add_turned(piece):
             c, k0, k1 = piece
-            sum_t[piece] = psum_z.tile([P, k1 - k0, P], F32, name="sum_t")
+            sum_t[piece] = psum.tile([P, k1 - k0, P], F32, name="sum_t", tag="bank")
             steps = [(part, k) for part in (bottom[piece], top[piece]) for k in range(k1 - k0)]
             for i, (part, k) in enumerate(steps):
                 nc.tensor.matmul(
@@ -215,7 +211,7 @@ def tile_list_cocoa_turning_features_kernel(
             nc.vector.scalar_tensor_tensor(
                 larger[:], top[piece][:], gain_col[:, c : c + 1], gained[piece][:], ALU.mult, ALU.max
             )
-            larger_t[piece] = psum_one.tile([P, k1 - k0, P], F32, name="larger_t", tag="larger_t")
+            larger_t[piece] = psum.tile([P, k1 - k0, P], F32, name="larger_t", tag="bank")
             for k in range(k1 - k0):
                 nc.tensor.transpose(larger_t[piece][:, k, :], larger[:, k * P : (k + 1) * P], ident[:])
 
@@ -227,43 +223,45 @@ def tile_list_cocoa_turning_features_kernel(
         def multiply(piece):
             c, k0, k1 = piece
             b, i = divmod(c, TILES_PER_PASS)
-            for k in range(k0, k1, 2):
-                j = k // 2
-                if i == 0:
-                    z_t[b, j] = held.tile([P, 2, 2, 2 * P], BF16, name=f"z_t{b}_{j}")
-                nc.vector.tensor_tensor(
-                    z_t[b, j][:, :, :, 64 * i : 64 * (i + 1)],
-                    larger_t[piece][:, k - k0 : k - k0 + 2, :].rearrange("p k (u x) -> p k u x", u=2),
-                    both_t[piece][:, k - k0 : k - k0 + 2, :].rearrange("p k (u x) -> p k u x", u=2),
-                    ALU.mult,
-                )
+            if (i, k0) == (0, 0):
+                z_t[b] = held.tile([P, M_CHUNKS * K_PASS], BF16, name=f"z_t{b}")
+            nc.vector.tensor_tensor(
+                z_t[b][:, k0 * K_PASS : k1 * K_PASS].rearrange("p (k r) -> p k r", r=K_PASS)[:, :, i * P : (i + 1) * P],
+                larger_t[piece][:],
+                both_t[piece][:],
+                ALU.mult,
+            )
 
-        def weave_z(b, j):
-            words = z_t[b, j][:].rearrange("p k u x -> p (k u x)").bitcast(F32)
-            turned = psum_lin.tile([P, 2, 2, P], F32, name="turned", tag="acc")
-            for k in range(2):
+        def weave_z(b, k0, k1):
+            turned = psum.tile([P, k1 - k0, 2, P], F32, name="turned", tag="bank")
+            for k in range(k0, k1):
+                words = z_t[b][:, k * K_PASS : (k + 1) * K_PASS].bitcast(F32)
                 for u in range(2):
-                    at = (2 * k + u) * P
-                    nc.tensor.transpose(turned[:, k, u, :], words[:, at : at + P], ident[:])
-            woven[b, j] = held.tile([P, M_HALF * PACK], BF16, name=f"woven{b}_{j}", align_bytes=64)
+                    nc.tensor.transpose(turned[:, k - k0, u, :], words[:, u : 2 * P : 2], ident[:])
+            woven[b, k0] = held.tile([P, (k1 - k0) * K_PASS], BF16, name=f"woven{b}_{k0}", align_bytes=64)
             nc.scalar.copy(
-                woven[b, j][:].bitcast(F32).rearrange("p (k m u) -> p k m u", k=2, u=2),
+                woven[b, k0][:].bitcast(F32).rearrange("p (k m u) -> p k m u", m=P, u=2),
                 turned[:].rearrange("p k u m -> p k m u"),
             )
 
-        def quantise_z(b, j):
-            at = ACT_AT + 4 * S + 4 * M_HALF * (2 * b + j)
-            codes = reused.tile([P, M_HALF], U32, name=f"z_codes{b}_{j}", align_bytes=64, offset=at)
-            scales = held.tile([P, M_HALF], U8, name=f"z_scales{b}_{j}", align_bytes=64)
-            nc.vector.quantize_mx(out=codes[:].bitcast(FP8X4), scales=scales[:], in_=woven[b, j][:])
-            z_q[b, j] = (codes, scales)
+        def quantise_z(b, k0, k1):
+            if k0 == 0:
+                at = ACT_AT + 4 * S + 4 * PAIRS * b
+                codes = reused.tile([P, PAIRS], U32, name=f"z_codes{b}", align_bytes=64, offset=at)
+                scales = held.tile([P, PAIRS], U8, name=f"z_scales{b}", align_bytes=64)
+                z_q[b] = (codes, scales)
+            codes, scales = z_q[b]
+            nc.vector.quantize_mx(
+                out=codes[:, k0 * P : k1 * P].bitcast(FP8X4), scales=scales[:, k0 * P : k1 * P], in_=woven[b, k0][:]
+            )
 
         last = TILES - 1
-        pieces = [(c, 0, M_CHUNKS) for c in range(last)] + [(last, 0, 2), (last, 2, M_CHUNKS)]
-        quantise_w1(0, 1)
-        first_stage(0)
-        quantise_w1(1, K_PASSES)
-        quantise_w1(2, 1)
+        pieces = [(c, 0, M_CHUNKS) for c in range(last)] + [(last, k0, k1) for k0, k1 in LAST_CUTS]
+        round_w1(0)
+        first_product(0)
+        take_gelu(0)
+        round_w1(1, 1)
+        first_product(1)
         for i, piece in enumerate(pieces):
             c = piece[0]
             gather_pairs(piece)
@@ -272,39 +270,47 @@ def tile_list_cocoa_turning_features_kernel(
                 multiply(pieces[i - 1])
             take_larger(piece)
             if c + 1 < TILES:
-                first_stage(c + 1)
+                take_gelu(c + 1)
+            if c + 2 < TILES:
+                if c == 0:
+                    round_w1(2)
+                first_product(c + 2)
             if c + 3 < TILES:
-                quantise_w1(c + 3, 1)
+                round_w1(c + 3)
             take_tanh(piece)
-            if c == TILES_PER_PASS + 1:
-                weave_z(0, 0)
-                weave_z(0, 1)
-        weave_z(1, 0)
+            if c == last - 1:
+                weave_z(0, 0, 2)
+                weave_z(0, 2, 4)
         multiply(pieces[-1])
-        weave_z(1, 1)
-        quantise_z(1, 0)
-        quantise_z(1, 1)
-        quantise_z(0, 0)
-        quantise_z(0, 1)
+        for k0, k1 in LAST_CUTS:
+            weave_z(1, k0, k1)
+        for k0, k1 in LAST_CUTS:
+            quantise_z(1, k0, k1)
+        quantise_z(0, 0, 2)
+        quantise_z(0, 2, 4)
 
         y = {}
 
         def second_stage(n):
             y[n] = held.tile([P, PAIRS], F32, name=f"y{n}")
-            for j in range(2):
-                acc = psum_lin.tile([P, M_HALF], F32, name="y_acc", tag="acc")
-                for b in range(R_PASSES):
-                    codes, scales = z_q[b, j]
+            groups = (LAST_CUTS[:-1], LAST_CUTS[-1:]) if n == 0 else (((0, M_CHUNKS),),)
+            for cuts in groups:
+                lo, hi = cuts[0][0] * P, cuts[-1][1] * P
+                acc = psum.tile([P, hi - lo], F32, name="y_acc", tag="sums")
+                order = range(R_PASSES) if n == 0 else reversed(range(R_PASSES))
+                steps = [(b, k0 * P, k1 * P) for b in order for k0, k1 in cuts]
+                for i, (b, m0, m1) in enumerate(steps):
+                    codes, scales = z_q[b]
                     nc.tensor.matmul_mx(
-                        out=acc[:],
+                        out=acc[:, m0 - lo : m1 - lo],
                         lhsT=w2_w[:, b, 2 * n * P : 2 * (n + 1) * P].bitcast(FP4X4),
                         lhsT_scale=w2_s[:, b, n * P : (n + 1) * P],
-                        rhs=codes[:].bitcast(FP8X4),
-                        rhs_scale=scales[:],
-                        start=(b == 0),
-                        stop=(b == R_PASSES - 1),
+                        rhs=codes[:, m0:m1].bitcast(FP8X4),
+                        rhs_scale=scales[:, m0:m1],
+                        start=(i == 0),
+                        stop=(i == len(steps) - 1),
                     )
-                nc.scalar.copy(y[n][:, j * M_HALF : (j + 1) * M_HALF], acc[:])
+                nc.scalar.copy(y[n][:, lo:hi], acc[:])
 
         def gather_later(n):
             later = ring3.tile([P, DIFFS], F32, name="later")

@@ -312,18 +312,13 @@ def tile_list_cocoa_turning_features_kernel(
                     )
                 nc.scalar.copy(y[n][:, lo:hi], acc[:])
 
-        def gather_later(n):
-            later = ring3.tile([P, DIFFS], F32, name="later")
-            nc.vector.tensor_copy(later[:], y[n][:].indirect(p4[:]))
-            return later
-
-        second_stage(0)
-        later = gather_later(0)
         for n in range(N_TILES):
-            if n + 1 < N_TILES:
-                second_stage(n + 1)
-                upcoming = gather_later(n + 1)
+            second_stage(n)
+            earlier = ring3.tile([P, DIFFS], F32, name="earlier")
+            nc.vector.tensor_copy(earlier[:], y[n][:].indirect(p3[:]))
+            later = ring3.tile([P, DIFFS], F32, name="later")
             diff = ring3.tile([P, DIFFS], F32, name="diff")
-            nc.vector.tensor_tensor(diff[:], y[n][:].indirect(p3[:]), later[:], ALU.subtract)
+            nc.vector.tensor_copy(later[:], y[n][:].indirect(p4[:]))
+            engine = nc.gpsimd if n + 1 < N_TILES else nc.vector
+            engine.tensor_tensor(diff[:], earlier[:], later[:], ALU.subtract)
             nc.sync.dma_start(out[n * P : (n + 1) * P, :], diff[:])
-            later = upcoming

from contextlib import ExitStack

import concourse.mybir as mybir
from concourse.masks import make_identity

K, H, N, T, S, PAIRS, DIFFS = 1536, 1024, 768, 4096, 1024, 512, 256
FLOPS = 2 * K * H * S + 2 * H * N * PAIRS

F32 = mybir.dt.float32
BF16 = mybir.dt.bfloat16
I32 = mybir.dt.int32
U32 = mybir.dt.uint32
U16 = mybir.dt.uint16
U8 = mybir.dt.uint8
FP8X4 = mybir.dt.float8_e4m3fn_x4
FP4X4 = mybir.dt.float4_e2m1fn_x4
ALU = mybir.AluOpType
ACT = mybir.ActivationFunctionType

P = 128
PACK = 4
K_PASS = P * PACK
K_PASSES = K // K_PASS
R_PASSES = H // K_PASS
TILES = H // P
TILES_PER_PASS = K_PASS // P
BANK = 512
HALVES = S // BANK
M_CHUNKS = PAIRS // P
M_HALF = PAIRS // 2
N_TILES = N // P
LAST_CUTS = ((0, 2), (2, 3), (3, 4))
ACT_AT = 5 * T
W1_CHUNKS = (1, 1, 1, 1, 2, 2)


def tile_list_cocoa_turning_features_kernel(
    tc, tab_words, tab_scales, offs, pos1, pos2, pos3, pos4, w1, gain, w2_words, w2_scales, out
):
    nc = tc.nc
    with ExitStack() as ctx:
        held = ctx.enter_context(tc.tile_pool(name="held", bufs=1))
        ring2 = ctx.enter_context(tc.tile_pool(name="ring2", bufs=2))
        ring3 = ctx.enter_context(tc.tile_pool(name="ring3", bufs=3))
        reused = ctx.enter_context(tc.tile_pool(name="reused", bufs=1))
        psum = ctx.enter_context(tc.psum_pool(name="psum", bufs=4))

        def load_list(src, name):
            tile = held.tile(list(src.shape), U16, name=name)
            nc.sync.dma_start(tile[:], src)
            return tile

        def load_table_words(a):
            if a == K_PASSES - 1:
                tile = reused.tile([P, T], I32, name=f"tab_w{a}", align_bytes=64, offset=0)
            else:
                tile = held.tile([P, T], I32, name=f"tab_w{a}", align_bytes=64)
            nc.sync.dma_start(tile[:], tab_words[a].rearrange("p t i -> p (t i)").bitcast(I32))
            return tile

        tab_s = reused.tile([P, T // 4], I32, name="tab_s", align_bytes=64, offset=4 * T)
        nc.vector.memset(tab_s[:], 0)
        w2_s = held.tile([P, R_PASSES, N], U8, name="w2_s", align_bytes=64)
        nc.vector.memset(w2_s[:].rearrange("p a n -> p (a n)").bitcast(I32), 0)
        for quad in range(4):
            nc.gpsimd.dma_start(
                tab_s[32 * quad : 32 * quad + 4 * K_PASSES, :],
                tab_scales[:, 4 * quad : 4 * quad + 4, :].bitcast(I32),
            )

        tab_w = [load_table_words(0)]
        idx = load_list(offs, "idx")
        tab_w.append(load_table_words(1))
        p1 = load_list(pos1, "p1")
        p2 = load_list(pos2, "p2")
        gain_rows = held.tile([TILES, P], F32, name="gain_rows")
        nc.sync.dma_start(gain_rows[:], gain.rearrange("(c r) -> c r", r=P))

        w1_raw = []
        first = 0
        for width in W1_CHUNKS:
            raw = held.tile([P, K_PASSES, PACK, width * P], F32, name=f"w1_raw{first}")
            for a in range(K_PASSES):
                rows = w1[a * K_PASS : (a + 1) * K_PASS, first * P : (first + width) * P]
                nc.sync.dma_start(raw[:, a], rows.rearrange("(p j) r -> p j r", j=PACK))
            w1_raw.extend(raw[:, :, :, i * P : (i + 1) * P] for i in range(width))
            if first == 0:
                p3 = load_list(pos3, "p3")
                tab_w.append(load_table_words(K_PASSES - 1))
            first = first + width

        p4 = load_list(pos4, "p4")
        w2_w = held.tile([P, R_PASSES, 2 * N], U8, name="w2_w", align_bytes=64)
        nc.sync.dma_start(w2_w[:].bitcast(I32), w2_words.rearrange("a p c -> p a c").bitcast(I32))
        for quad in range(4):
            nc.sync.dma_start(
                w2_s[32 * quad : 32 * quad + 4, :, :].bitcast(I32),
                w2_scales[:, 4 * quad : 4 * quad + 4, :].rearrange("a r c -> r a c").bitcast(I32),
            )

        ident = held.tile([P, P], F32, name="ident")
        make_identity(nc, ident[:])
        gain_sq = held.tile([P, P], F32, name="gain_sq")
        nc.gpsimd.memset(gain_sq[:], 0.0)
        nc.vector.tensor_copy(gain_sq[0:TILES, :], gain_rows[:])
        gain_t = psum.tile([P, M_CHUNKS, P], F32, name="gain_t", tag="bank")
        nc.tensor.transpose(gain_t[:, 0, :], gain_sq[:], ident[:])
        gain_col = held.tile([P, TILES], F32, name="gain_col")
        nc.vector.tensor_copy(gain_col[:], gain_t[:, 0, 0:TILES])

        got_w = {}
        got_s = held.tile([P, S], U8, name="got_s", align_bytes=64)
        cols = BANK // 16

        def gather_words(a):
            for h in range(HALVES):
                if a == K_PASSES - 1:
                    at = 4 * T + 4 * BANK * h
                    tile = reused.tile([P, BANK], U32, name=f"got_w{a}_{h}", align_bytes=64, offset=at)
                else:
                    tile = held.tile([P, BANK], U32, name=f"got_w{a}_{h}", align_bytes=64)
                window = tab_w[a][:].bitcast(U32)
                nc.vector.tensor_copy(tile[:], window.indirect(idx[:, h * cols : (h + 1) * cols]))
                got_w[a, h] = tile

        for a in range(K_PASSES - 1):
            gather_words(a)
        nc.vector.tensor_copy(got_s[:], tab_s[:].bitcast(U8).indirect(idx[:]))
        gather_words(K_PASSES - 1)

        w1_q, act, top, bottom, gained, larger_t, both_t, z_t, z_q = {}, {}, {}, {}, {}, {}, {}, {}, {}
        sum_t, woven, rounded, lin = {}, {}, {}, {}

        def round_w1(c, step=K_PASSES):
            if c == 1:
                rounded = held.tile([P, K_PASSES, K_PASS], BF16, name="w1_bf_second", tag="handed_on0", align_bytes=64)
            else:
                rounded = ring2.tile([P, K_PASSES, K_PASS], BF16, name="w1_bf", align_bytes=64)
            if c < W1_CHUNKS[0]:
                codes = held.tile([P, K_PASSES * P], U32, name=f"w1_codes_first{c}", align_bytes=64)
            else:
                codes = reused.tile([P, K_PASSES * P], U32, name="w1_codes", align_bytes=64, offset=0, bufs=2)
            scales = ring2.tile([P, K_PASSES * P], U8, name="w1_scales", align_bytes=64)
            for a0 in range(0, K_PASSES, step):
                a1 = a0 + step
                nc.scalar.copy(
                    rounded[:, a0:a1, :].rearrange("p a (g i j) -> p a g j i", i=4, j=PACK),
                    w1_raw[c][:, a0:a1].rearrange("p a j (g i) -> p a g j i", i=4),
                )
                nc.vector.quantize_mx(
                    out=codes[:, a0 * P : a1 * P].bitcast(FP8X4),
                    scales=scales[:, a0 * P : a1 * P],
                    in_=rounded[:, a0:a1, :].rearrange("p a x -> p (a x)"),
                )
            w1_q[c] = (codes, scales)

        def first_product(c):
            codes, scales = w1_q[c]
            lin[c] = [psum.tile([P, BANK], F32, name="lin", tag="sums") for h in range(HALVES)]
            for a in range(K_PASSES):
                for h in range(HALVES):
                    nc.tensor.matmul_mx(
                        out=lin[c][h][:],
                        lhsT=codes[:, a * P : (a + 1) * P].bitcast(FP8X4),
                        lhsT_scale=scales[:, a * P : (a + 1) * P],
                        rhs=got_w[a, h][:].bitcast(FP8X4),
                        rhs_scale=got_s[4 * a :, h * BANK : (h + 1) * BANK],
                        start=(a == 0),
                        stop=(a == K_PASSES - 1),
                    )

        def take_gelu(c):
            act[c] = reused.tile([P, S], F32, name="act", offset=ACT_AT, bufs=2)
            for h in range(HALVES):
                nc.scalar.activation(act[c][:, h * BANK : (h + 1) * BANK], lin[c][h][:], ACT.Gelu_apprx_tanh)

        def gather_pairs(piece):
            c, k0, k1 = piece
            width = (k1 - k0) * P
            entries = slice(k0 * P // 16, k1 * P // 16)
            bottom[piece] = ring3.tile([P, width], F32, name="bottom")
            nc.vector.tensor_copy(bottom[piece][:], act[c][:].indirect(p2[:, entries]))
            if k1 < M_CHUNKS:
                gained[piece] = held.tile([P, width], F32, name="gained_early", tag=f"handed_on{k1}", align_bytes=64)
            else:
                gained[piece] = ring2.tile([P, width], F32, name="gained")
            nc.scalar.activation(gained[piece][:], bottom[piece][:], ACT.Copy, scale=gain_col[:, c : c + 1])
            if k0 > 0 or c == 0:
                top[piece] = held.tile([P, width], F32, name="top_late", tag=f"handed_on{k0}", align_bytes=64)
            else:
                top[piece] = ring2.tile([P, width], F32, name="top")
            nc.vector.tensor_copy(top[piece][:], act[c][:].indirect(p1[:, entries]))

        def add_turned(piece):
            c, k0, k1 = piece
            sum_t[piece] = psum.tile([P, k1 - k0, P], F32, name="sum_t", tag="bank")
            steps = [(part, k) for part in (bottom[piece], top[piece]) for k in range(k1 - k0)]
            for i, (part, k) in enumerate(steps):
                nc.tensor.matmul(
                    sum_t[piece][:, k, :],
                    part[:, k * P : (k + 1) * P],
                    ident[:],
                    start=(i == 0),
                    stop=(i == len(steps) - 1),
                    is_transpose=True,
                )

        def take_larger(piece):
            c, k0, k1 = piece
            larger = ring2.tile([P, (k1 - k0) * P], F32, name="larger")
            nc.vector.scalar_tensor_tensor(
                larger[:], top[piece][:], gain_col[:, c : c + 1], gained[piece][:], ALU.mult, ALU.max
            )
            larger_t[piece] = psum.tile([P, k1 - k0, P], F32, name="larger_t", tag="bank")
            for k in range(k1 - k0):
                nc.tensor.transpose(larger_t[piece][:, k, :], larger[:, k * P : (k + 1) * P], ident[:])

        def take_tanh(piece):
            c, k0, k1 = piece
            both_t[piece] = ring2.tile([P, k1 - k0, P], F32, name="both_t")
            nc.scalar.activation(both_t[piece][:], sum_t[piece][:], ACT.Tanh)

        def multiply(piece):
            c, k0, k1 = piece
            b, i = divmod(c, TILES_PER_PASS)
            if (i, k0) == (0, 0):
                z_t[b] = held.tile([P, M_CHUNKS * K_PASS], BF16, name=f"z_t{b}")
            nc.vector.tensor_tensor(
                z_t[b][:, k0 * K_PASS : k1 * K_PASS].rearrange("p (k r) -> p k r", r=K_PASS)[:, :, i * P : (i + 1) * P],
                larger_t[piece][:],
                both_t[piece][:],
                ALU.mult,
            )

        def weave_z(b, k0, k1):
            turned = psum.tile([P, k1 - k0, 2, P], F32, name="turned", tag="bank")
            for k in range(k0, k1):
                words = z_t[b][:, k * K_PASS : (k + 1) * K_PASS].bitcast(F32)
                for u in range(2):
                    nc.tensor.transpose(turned[:, k - k0, u, :], words[:, u : 2 * P : 2], ident[:])
            woven[b, k0] = held.tile([P, (k1 - k0) * K_PASS], BF16, name=f"woven{b}_{k0}", align_bytes=64)
            nc.scalar.copy(
                woven[b, k0][:].bitcast(F32).rearrange("p (k m u) -> p k m u", m=P, u=2),
                turned[:].rearrange("p k u m -> p k m u"),
            )

        def quantise_z(b, k0, k1):
            if k0 == 0:
                at = ACT_AT + 4 * S + 4 * PAIRS * b
                codes = reused.tile([P, PAIRS], U32, name=f"z_codes{b}", align_bytes=64, offset=at)
                scales = held.tile([P, PAIRS], U8, name=f"z_scales{b}", align_bytes=64)
                z_q[b] = (codes, scales)
            codes, scales = z_q[b]
            nc.vector.quantize_mx(
                out=codes[:, k0 * P : k1 * P].bitcast(FP8X4), scales=scales[:, k0 * P : k1 * P], in_=woven[b, k0][:]
            )

        last = TILES - 1
        pieces = [(c, 0, M_CHUNKS) for c in range(last)] + [(last, k0, k1) for k0, k1 in LAST_CUTS]
        round_w1(0)
        first_product(0)
        take_gelu(0)
        round_w1(1, 1)
        first_product(1)
        for i, piece in enumerate(pieces):
            c = piece[0]
            gather_pairs(piece)
            add_turned(piece)
            if i > 0:
                multiply(pieces[i - 1])
            take_larger(piece)
            if c + 1 < TILES:
                take_gelu(c + 1)
            if c + 2 < TILES:
                if c == 0:
                    round_w1(2)
                first_product(c + 2)
            if c + 3 < TILES:
                round_w1(c + 3)
            take_tanh(piece)
            if c == last - 1:
                weave_z(0, 0, 2)
                weave_z(0, 2, 4)
        multiply(pieces[-1])
        for k0, k1 in LAST_CUTS:
            weave_z(1, k0, k1)
        for k0, k1 in LAST_CUTS:
            quantise_z(1, k0, k1)
        quantise_z(0, 0, 2)
        quantise_z(0, 2, 4)

        y = {}

        def second_stage(n):
            y[n] = held.tile([P, PAIRS], F32, name=f"y{n}")
            groups = (LAST_CUTS[:-1], LAST_CUTS[-1:]) if n == 0 else (((0, M_CHUNKS),),)
            for cuts in groups:
                lo, hi = cuts[0][0] * P, cuts[-1][1] * P
                acc = psum.tile([P, hi - lo], F32, name="y_acc", tag="sums")
                order = range(R_PASSES) if n == 0 else reversed(range(R_PASSES))
                steps = [(b, k0 * P, k1 * P) for b in order for k0, k1 in cuts]
                for i, (b, m0, m1) in enumerate(steps):
                    codes, scales = z_q[b]
                    nc.tensor.matmul_mx(
                        out=acc[:, m0 - lo : m1 - lo],
                        lhsT=w2_w[:, b, 2 * n * P : 2 * (n + 1) * P].bitcast(FP4X4),
                        lhsT_scale=w2_s[:, b, n * P : (n + 1) * P],
                        rhs=codes[:, m0:m1].bitcast(FP8X4),
                        rhs_scale=scales[:, m0:m1],
                        start=(i == 0),
                        stop=(i == len(steps) - 1),
                    )
                nc.scalar.copy(y[n][:, lo:hi], acc[:])

        for n in range(N_TILES):
            second_stage(n)
            earlier = ring3.tile([P, DIFFS], F32, name="earlier")
            nc.vector.tensor_copy(earlier[:], y[n][:].indirect(p3[:]))
            later = ring3.tile([P, DIFFS], F32, name="later")
            diff = ring3.tile([P, DIFFS], F32, name="diff")
            nc.vector.tensor_copy(later[:], y[n][:].indirect(p4[:]))
            engine = nc.gpsimd if n + 1 < N_TILES else nc.vector
            engine.tensor_tensor(diff[:], earlier[:], later[:], ALU.subtract)
            nc.sync.dma_start(out[n * P : (n + 1) * P, :], diff[:])
